import numpy as np
import ml_dtypes


def mxq(x, axis, fmt="e4m3"):
    dtype, down = {"e4m3": (ml_dtypes.float8_e4m3fn, 7), "e5m2": (ml_dtypes.float8_e5m2, 14)}[fmt]
    v = np.moveaxis(np.asarray(x, np.float32).astype(ml_dtypes.bfloat16).astype(np.float64), axis, -1)
    blocks = v.reshape(v.shape[:-1] + (-1, 32))
    amax = np.abs(blocks).max(-1, keepdims=True)
    byte = np.maximum(np.where(amax > 0, np.frexp(amax)[1] - 1 + 127, 0) - down, 1)
    scale = np.exp2(byte - 127.0)
    codes = (blocks / scale).astype(np.float32).astype(dtype).astype(np.float64)
    return np.moveaxis((codes * scale).reshape(v.shape), -1, axis)


WIDE = False


def mx_kscale(k):
    if not WIDE:
        return np.ones(k)
    levels = np.array([10, -10, 5, -5, 0])
    if k % 512:
        return np.exp2(np.random.permutation(np.resize(levels, k // 32))).repeat(32)
    a = np.empty((k // 512, 16))
    for p in range(k // 512):
        a[p, :8] = np.random.permutation(np.resize(levels, 8))
        for g in range(8):
            far = levels[np.abs(levels - a[p, g]) >= 10]
            a[p, g + 8] = far[np.random.randint(len(far))]
    return np.exp2(a.ravel()).repeat(32)


def f64(x):
    return np.asarray(x).astype(np.float64)


def striped(idx):
    return np.tile(idx.reshape(-1, 16).T, (8, 1)).astype(np.uint16)


def unstriped(offs):
    return offs[:16].T.reshape(-1).astype(np.int64)


def silu(v):
    return v / (1.0 + np.exp(-np.maximum(v, -700.0)))


K, T, S, N = 1024, 2048, 512, 256
P = 2 ** 7


def setup_inputs():
    n = np.random.standard_normal
    s = mx_kscale(K)[:, None]
    return {
        "xT": (n((K, T)) * s).astype(np.float32),
        "mean": np.tile(0.3 * np.random.standard_normal(T), (P, 1)).astype(np.float32),
        "inv": np.tile(np.random.uniform(0.5, 2.0, T), (P, 1)).astype(np.float32),
        "gsum": n((N, 1)).astype(np.float32),
        "b": (0.3 * n((N, 1))).astype(np.float32),
        "w1": (n((K, N)) / np.sqrt(K) / s).astype(np.float32),
        "offs": striped(np.random.permutation(T)[:S]),
    }


def reference(xT, mean, inv, gsum, b, w1, offs):
    xq = mxq(f64(xT)[:, unstriped(offs)], 0, "e4m3")
    y = mxq(f64(w1), 0, "e4m3").T @ xq
    mg = f64(mean)[:1][:, unstriped(offs)]
    ig = f64(inv)[:1][:, unstriped(offs)]
    return silu((y - (f64(gsum) * mg)) * ig + f64(b))

@@ -1,0 +1,168 @@
+from contextlib import ExitStack
+
+import concourse.mybir as mybir
+from concourse.masks import make_identity
+
+K, T, S, N = 1024, 2048, 512, 256
+FLOPS = 2 * K * S * N
+BYTES = 4 * (K * T + 2 * T + 2 * N + K * N + N * S) + 2 * 128 * (S // 16)
+
+F32 = mybir.dt.float32
+BF16 = mybir.dt.bfloat16
+U32 = mybir.dt.uint32
+U16 = mybir.dt.uint16
+U8 = mybir.dt.uint8
+FP8X4 = mybir.dt.float8_e4m3fn_x4
+MULT = mybir.AluOpType.mult
+ADD = mybir.AluOpType.add
+SILU = mybir.ActivationFunctionType.Silu
+
+P = 128
+PACK = 4
+K_PASS = P * PACK
+PASSES = K // K_PASS
+BLOCKS = S // P
+HALF = S // 2
+
+
+def tile_picked_lnfold_silu_l_kernel(tc, xT, mean, inv, gsum, b, w1, offs, out):
+    nc = tc.nc
+    with ExitStack() as ctx:
+        keep = ctx.enter_context(tc.tile_pool(name="keep", bufs=1))
+        psum = ctx.enter_context(tc.psum_pool(name="psum", bufs=1))
+
+        offsets = keep.tile([P, S // 16], U16, name="offsets")
+        x_rows = xT.rearrange("(g p j) t -> g j p t", p=P, j=PACK)
+        w_rows = w1.rearrange("(g p j) n -> g p j n", p=P, j=PACK)
+        x_planes = [keep.tile([P, T], F32, name="x_plane%d" % i) for i in range(PASSES * PACK)]
+        w_raw = [keep.tile([P, PACK, N], F32, name="w_raw%d" % g) for g in range(PASSES)]
+        stat_rows = keep.tile([2, T], F32, name="stat_rows")
+        gsum_col = keep.tile([P, 2], F32, name="gsum_col")
+        b_col = keep.tile([P, 2], F32, name="b_col")
+
+        def load_x(i):
+            nc.sync.dma_start(out=x_planes[i][:], in_=x_rows[i // PACK, i % PACK])
+
+        load_x(0)
+        nc.sync.dma_start(offsets[:], offs)
+        nc.scalar.dma_start(out=stat_rows[0:1, :], in_=mean[0:1, :])
+        nc.scalar.dma_start(out=stat_rows[1:2, :], in_=inv[0:1, :])
+        nc.scalar.dma_start(out=gsum_col[:], in_=gsum.rearrange("(p t) o -> p (t o)", t=2))
+        nc.scalar.dma_start(out=b_col[:], in_=b.rearrange("(p t) o -> p (t o)", t=2))
+        for i in range(1, PACK):
+            load_x(i)
+        nc.sync.dma_start(out=w_raw[0][:], in_=w_rows[0])
+        for i in range(PACK, 2 * PACK):
+            load_x(i)
+        nc.sync.dma_start(out=w_raw[1][:], in_=w_rows[1])
+
+        ident = keep.tile([P, P], F32, name="ident")
+        make_identity(nc, ident[:])
+        warm = keep.tile([P, 1], F32, name="warm")
+        nc.scalar.activation(warm[:], ident[:, 0:1], SILU)
+
+        stat_window = keep.tile([P, T], F32, name="stat_window")
+        nc.vector.memset(stat_window[:], 0.0)
+        nc.scalar.copy(stat_window[0:2, :], stat_rows[:])
+
+        x_grouped = [keep.tile([P, S, PACK], BF16, name="x_grouped%d" % g, align_bytes=64) for g in range(PASSES)]
+        x_codes = [keep.tile([P, S], U32, name="x_codes%d" % g, align_bytes=64) for g in range(PASSES)]
+        x_scales = [keep.tile([P, S], U8, name="x_scales%d" % g, align_bytes=64) for g in range(PASSES)]
+        w_grouped = [keep.tile([P, N, PACK], BF16, name="w_grouped%d" % g, align_bytes=64) for g in range(PASSES)]
+        w_codes = [keep.tile([P, N], U32, name="w_codes%d" % g, align_bytes=64) for g in range(PASSES)]
+        w_scales = [keep.tile([P, N], U8, name="w_scales%d" % g, align_bytes=64) for g in range(PASSES)]
+        acc = [psum.tile([P, N], F32, name="acc%d" % blk) for blk in range(BLOCKS)]
+
+        def gather_x(i, lo, hi):
+            nc.vector.tensor_copy(
+                x_grouped[i // PACK][:, lo:hi, i % PACK],
+                x_planes[i][:].indirect(offsets[:, lo // 16 : hi // 16]),
+            )
+
+        def quantize_x(g, lo, hi):
+            nc.vector.quantize_mx(
+                out=x_codes[g][:, lo:hi].bitcast(FP8X4),
+                scales=x_scales[g][:, lo:hi],
+                in_=x_grouped[g][:].rearrange("p s j -> p (s j)")[:, PACK * lo : PACK * hi],
+            )
+
+        def group_w(g):
+            nc.scalar.copy(
+                w_grouped[g][:].rearrange("p (c i) j -> p c j i", i=4),
+                w_raw[g][:].rearrange("p j (c i) -> p c j i", i=4),
+            )
+
+        def quantize_w(g):
+            nc.vector.quantize_mx(
+                out=w_codes[g][:].bitcast(FP8X4),
+                scales=w_scales[g][:],
+                in_=w_grouped[g][:].rearrange("p n j -> p (n j)"),
+            )
+
+        def multiply(g, blk):
+            cols = slice(blk * P, (blk + 1) * P)
+            nc.tensor.matmul_mx(
+                out=acc[blk][:],
+                lhsT=x_codes[g][:, cols].bitcast(FP8X4),
+                lhsT_scale=x_scales[g][:, cols],
+                rhs=w_codes[g][:].bitcast(FP8X4),
+                rhs_scale=w_scales[g][:],
+                start=(g == 0),
+                stop=(g == PASSES - 1),
+            )
+
+        gather_x(0, 0, S)
+        stat_picked = keep.tile([P, S], F32, name="stat_picked")
+        nc.vector.tensor_copy(stat_picked[:], stat_window[:].indirect(offsets[:]))
+        stat_turned = psum.tile([P, BLOCKS, P], F32, name="stat_turned", tag="turn0")
+        for blk in range(BLOCKS):
+            nc.tensor.transpose(stat_turned[:, blk, :], stat_picked[:, blk * P : (blk + 1) * P], ident[:])
+        stats = keep.tile([P, BLOCKS, 2], F32, name="stats")
+        nc.scalar.copy(stats[:], stat_turned[:, :, 0:2])
+        gsum_rows = psum.tile([P, 2, P], F32, name="gsum_rows", tag="turn1")
+        b_turned = psum.tile([P, 2, P], F32, name="b_turned", tag="turn2")
+        for t in range(2):
+            nc.tensor.transpose(gsum_rows[:, t, :], gsum_col[:, t : t + 1].to_broadcast([P, P]), ident[:])
+            nc.tensor.transpose(b_turned[:, t, :], b_col[:, t : t + 1].to_broadcast([P, P]), ident[:])
+        b_rows = keep.tile([P, P, 2], F32, name="b_rows")
+        nc.scalar.copy(b_rows[:], b_turned[:].rearrange("p t n -> p n t"))
+
+        gather_x(1, 0, S)
+        shift = keep.tile([P, BLOCKS], F32, name="shift")
+        nc.vector.scalar_tensor_tensor(shift[:], stats[:, :, 0], -1.0, stats[:, :, 1], MULT, MULT)
+        gather_x(2, 0, S)
+        offset_term = [keep.tile([P, P, 2], F32, name="offset_term%d" % blk) for blk in range(BLOCKS)]
+        for blk in range(BLOCKS):
+            nc.vector.scalar_tensor_tensor(
+                offset_term[blk][:], gsum_rows[:].rearrange("p t n -> p n t"), shift[:, blk : blk + 1], b_rows[:], MULT, ADD
+            )
+        gather_x(3, 0, S)
+        group_w(0)
+        gather_x(4, 0, S)
+        quantize_x(0, 0, S)
+        quantize_w(0)
+        for blk in range(BLOCKS):
+            multiply(0, blk)
+        gather_x(5, 0, S)
+        gather_x(6, 0, S)
+        gather_x(7, 0, HALF)
+        gather_x(7, HALF, S)
+        group_w(1)
+        quantize_x(1, 0, HALF)
+        quantize_x(1, HALF, S)
+        quantize_w(1)
+        for blk in range(BLOCKS):
+            multiply(1, blk)
+
+        out_view = out.rearrange("(t p) s -> p t s", p=P)
+        for blk in range(BLOCKS):
+            pre = keep.tile([P, N], F32, name="pre%d" % blk)
+            nc.vector.scalar_tensor_tensor(
+                pre[:], acc[blk][:], stats[:, blk, 1:2], offset_term[blk][:].rearrange("p n t -> p (n t)"), MULT, ADD
+            )
+            turned = psum.tile([P, 2, P], F32, name="turned%d" % blk, tag="turn%d" % blk)
+            for t in range(2):
+                nc.tensor.transpose(turned[:, t, :], pre[:, t * P : (t + 1) * P], ident[:])
+            result = keep.tile([P, 2, P], F32, name="result%d" % blk)
+            nc.scalar.activation(result[:], turned[:], SILU)
+            nc.sync.dma_start(out=out_view[:, :, blk * P : (blk + 1) * P], in_=result[:])

@@ -23,6 +23,7 @@ K_PASS = P * PACK
 PASSES = K // K_PASS
 BLOCKS = S // P
 HALF = S // 2
+RUN = T // P
 
 
 def tile_picked_lnfold_silu_l_kernel(tc, xT, mean, inv, gsum, b, w1, offs, out):
@@ -36,7 +37,7 @@ def tile_picked_lnfold_silu_l_kernel(tc, xT, mean, inv, gsum, b, w1, offs, out):
         w_rows = w1.rearrange("(g p j) n -> g p j n", p=P, j=PACK)
         x_planes = [keep.tile([P, T], F32, name="x_plane%d" % i) for i in range(PASSES * PACK)]
         w_raw = [keep.tile([P, PACK, N], F32, name="w_raw%d" % g) for g in range(PASSES)]
-        stat_rows = keep.tile([2, T], F32, name="stat_rows")
+        stat_runs = keep.tile([P, RUN + P], F32, name="stat_runs")
         gsum_col = keep.tile([P, 2], F32, name="gsum_col")
         b_col = keep.tile([P, 2], F32, name="b_col")
 
@@ -45,8 +46,8 @@ def tile_picked_lnfold_silu_l_kernel(tc, xT, mean, inv, gsum, b, w1, offs, out):
 
         load_x(0)
         nc.sync.dma_start(offsets[:], offs)
-        nc.scalar.dma_start(out=stat_rows[0:1, :], in_=mean[0:1, :])
-        nc.scalar.dma_start(out=stat_rows[1:2, :], in_=inv[0:1, :])
+        nc.scalar.dma_start(out=stat_runs[:, 0:RUN], in_=mean[0:1, :].rearrange("o (p c) -> (o p) c", c=RUN))
+        nc.scalar.dma_start(out=stat_runs[:, RUN : 2 * RUN], in_=inv[0:1, :].rearrange("o (p c) -> (o p) c", c=RUN))
         nc.scalar.dma_start(out=gsum_col[:], in_=gsum.rearrange("(p t) o -> p (t o)", t=2))
         nc.scalar.dma_start(out=b_col[:], in_=b.rearrange("(p t) o -> p (t o)", t=2))
         for i in range(1, PACK):
@@ -62,12 +63,20 @@ def tile_picked_lnfold_silu_l_kernel(tc, xT, mean, inv, gsum, b, w1, offs, out):
         nc.scalar.activation(warm[:], ident[:, 0:1], SILU)
 
         stat_window = keep.tile([P, T], F32, name="stat_window")
-        nc.vector.memset(stat_window[:], 0.0)
-        nc.scalar.copy(stat_window[0:2, :], stat_rows[:])
+        nc.vector.memset(stat_runs[:, 2 * RUN :], 0.0)
+        for q in range(RUN // 4):
+            bank = psum.tile([P, 4, P], F32, name="bank", tag="turn%d" % q)
+            for c in range(4):
+                nc.tensor.transpose(bank[:, c, :], stat_runs[:, 4 * q + c : 4 * q + c + P], ident[:])
+            nc.scalar.copy(
+                stat_window[:].rearrange("p (n c) -> p n c", c=RUN)[:, :, 4 * q : 4 * q + 4],
+                bank[:].rearrange("p c n -> p n c"),
+            )
 
         x_grouped = [keep.tile([P, S, PACK], BF16, name="x_grouped%d" % g, align_bytes=64) for g in range(PASSES)]
-        x_codes = [keep.tile([P, S], U32, name="x_codes%d" % g, align_bytes=64) for g in range(PASSES)]
-        x_scales = [keep.tile([P, S], U8, name="x_scales%d" % g, align_bytes=64) for g in range(PASSES)]
+        x_picked = keep.tile([P, PACK, S], F32, name="x_picked")
+        x_codes = {}
+        x_scales = {}
         w_grouped = [keep.tile([P, N, PACK], BF16, name="w_grouped%d" % g, align_bytes=64) for g in range(PASSES)]
         w_codes = [keep.tile([P, N], U32, name="w_codes%d" % g, align_bytes=64) for g in range(PASSES)]
         w_scales = [keep.tile([P, N], U8, name="w_scales%d" % g, align_bytes=64) for g in range(PASSES)]
@@ -79,12 +88,21 @@ def tile_picked_lnfold_silu_l_kernel(tc, xT, mean, inv, gsum, b, w1, offs, out):
                 x_planes[i][:].indirect(offsets[:, lo // 16 : hi // 16]),
             )
 
-        def quantize_x(g, lo, hi):
+        def pick_x(j):
+            nc.vector.tensor_copy(x_picked[:, j, :], x_planes[j][:].indirect(offsets[:]))
+
+        def quantize_x(g, lo, hi, tag):
+            codes = keep.tile([P, hi - lo], U32, name="x_codes", tag=tag, align_bytes=64)
+            scales = keep.tile([P, hi - lo], U8, name="x_scales", tag="x_scales%d_%d" % (g, lo), align_bytes=64)
             nc.vector.quantize_mx(
-                out=x_codes[g][:, lo:hi].bitcast(FP8X4),
-                scales=x_scales[g][:, lo:hi],
+                out=codes[:].bitcast(FP8X4),
+                scales=scales[:],
                 in_=x_grouped[g][:].rearrange("p s j -> p (s j)")[:, PACK * lo : PACK * hi],
             )
+            for blk in range(lo // P, hi // P):
+                cols = slice(blk * P - lo, (blk + 1) * P - lo)
+                x_codes[g, blk] = codes[:, cols]
+                x_scales[g, blk] = scales[:, cols]
 
         def group_w(g):
             nc.scalar.copy(
@@ -100,46 +118,48 @@ def tile_picked_lnfold_silu_l_kernel(tc, xT, mean, inv, gsum, b, w1, offs, out):
             )
 
         def multiply(g, blk):
-            cols = slice(blk * P, (blk + 1) * P)
             nc.tensor.matmul_mx(
                 out=acc[blk][:],
-                lhsT=x_codes[g][:, cols].bitcast(FP8X4),
-                lhsT_scale=x_scales[g][:, cols],
+                lhsT=x_codes[g, blk].bitcast(FP8X4),
+                lhsT_scale=x_scales[g, blk],
                 rhs=w_codes[g][:].bitcast(FP8X4),
                 rhs_scale=w_scales[g][:],
                 start=(g == 0),
                 stop=(g == PASSES - 1),
             )
 
-        gather_x(0, 0, S)
+        pick_x(0)
         stat_picked = keep.tile([P, S], F32, name="stat_picked")
         nc.vector.tensor_copy(stat_picked[:], stat_window[:].indirect(offsets[:]))
         stat_turned = psum.tile([P, BLOCKS, P], F32, name="stat_turned", tag="turn0")
         for blk in range(BLOCKS):
             nc.tensor.transpose(stat_turned[:, blk, :], stat_picked[:, blk * P : (blk + 1) * P], ident[:])
         stats = keep.tile([P, BLOCKS, 2], F32, name="stats")
-        nc.scalar.copy(stats[:], stat_turned[:, :, 0:2])
-        gsum_rows = psum.tile([P, 2, P], F32, name="gsum_rows", tag="turn1")
-        b_turned = psum.tile([P, 2, P], F32, name="b_turned", tag="turn2")
+        nc.scalar.copy(stats[:], stat_turned[:, :, 0 : 2 * RUN : RUN])
+        spread = psum.tile([P, 2, 2, P], F32, name="spread", tag="turn1")
         for t in range(2):
-            nc.tensor.transpose(gsum_rows[:, t, :], gsum_col[:, t : t + 1].to_broadcast([P, P]), ident[:])
-            nc.tensor.transpose(b_turned[:, t, :], b_col[:, t : t + 1].to_broadcast([P, P]), ident[:])
-        b_rows = keep.tile([P, P, 2], F32, name="b_rows")
-        nc.scalar.copy(b_rows[:], b_turned[:].rearrange("p t n -> p n t"))
+            nc.tensor.transpose(spread[:, 0, t, :], gsum_col[:, t : t + 1].to_broadcast([P, P]), ident[:])
+            nc.tensor.transpose(spread[:, 1, t, :], b_col[:, t : t + 1].to_broadcast([P, P]), ident[:])
+        rows = keep.tile([P, 2, N], F32, name="rows")
+        nc.scalar.copy(rows[:].rearrange("p v (n t) -> p v n t", t=2), spread[:].rearrange("p v t n -> p v n t"))
 
-        gather_x(1, 0, S)
+        pick_x(1)
         shift = keep.tile([P, BLOCKS], F32, name="shift")
         nc.vector.scalar_tensor_tensor(shift[:], stats[:, :, 0], -1.0, stats[:, :, 1], MULT, MULT)
-        gather_x(2, 0, S)
-        offset_term = [keep.tile([P, P, 2], F32, name="offset_term%d" % blk) for blk in range(BLOCKS)]
+        pick_x(2)
+        offset_term = [keep.tile([P, N], F32, name="offset_term%d" % blk) for blk in range(BLOCKS)]
         for blk in range(BLOCKS):
             nc.vector.scalar_tensor_tensor(
-                offset_term[blk][:], gsum_rows[:].rearrange("p t n -> p n t"), shift[:, blk : blk + 1], b_rows[:], MULT, ADD
+                offset_term[blk][:], rows[:, 0, :], shift[:, blk : blk + 1], rows[:, 1, :], MULT, ADD
             )
-        gather_x(3, 0, S)
+        pick_x(3)
+        nc.scalar.copy(
+            x_grouped[0][:].rearrange("p (c i) j -> p c j i", i=4),
+            x_picked[:].rearrange("p j (c i) -> p c j i", i=4),
+        )
         group_w(0)
         gather_x(4, 0, S)
-        quantize_x(0, 0, S)
+        quantize_x(0, 0, S, "x_codes0")
         quantize_w(0)
         for blk in range(BLOCKS):
             multiply(0, blk)
@@ -148,9 +168,9 @@ def tile_picked_lnfold_silu_l_kernel(tc, xT, mean, inv, gsum, b, w1, offs, out):
         gather_x(7, 0, HALF)
         gather_x(7, HALF, S)
         group_w(1)
-        quantize_x(1, 0, HALF)
-        quantize_x(1, HALF, S)
+        quantize_x(1, 0, HALF, "x_codes1")
         quantize_w(1)
+        quantize_x(1, HALF, S, "w_grouped1")
         for blk in range(BLOCKS):
             multiply(1, blk)
 
@@ -158,11 +178,12 @@ def tile_picked_lnfold_silu_l_kernel(tc, xT, mean, inv, gsum, b, w1, offs, out):
         for blk in range(BLOCKS):
             pre = keep.tile([P, N], F32, name="pre%d" % blk)
             nc.vector.scalar_tensor_tensor(
-                pre[:], acc[blk][:], stats[:, blk, 1:2], offset_term[blk][:].rearrange("p n t -> p (n t)"), MULT, ADD
+                pre[:], acc[blk][:], stats[:, blk, 1:2], offset_term[blk][:], MULT, ADD
             )
             turned = psum.tile([P, 2, P], F32, name="turned%d" % blk, tag="turn%d" % blk)
             for t in range(2):
                 nc.tensor.transpose(turned[:, t, :], pre[:, t * P : (t + 1) * P], ident[:])
             result = keep.tile([P, 2, P], F32, name="result%d" % blk)
             nc.scalar.activation(result[:], turned[:], SILU)
-            nc.sync.dma_start(out=out_view[:, :, blk * P : (blk + 1) * P], in_=result[:])
+            queue = nc.scalar if blk == BLOCKS - 1 else nc.sync
+            queue.dma_start(out=out_view[:, :, blk * P : (blk + 1) * P], in_=result[:])

@@ -30,32 +30,42 @@ def tile_picked_lnfold_silu_l_kernel(tc, xT, mean, inv, gsum, b, w1, offs, out):
     nc = tc.nc
     with ExitStack() as ctx:
         keep = ctx.enter_context(tc.tile_pool(name="keep", bufs=1))
+        shared = ctx.enter_context(tc.tile_pool(name="shared", bufs=1))
         psum = ctx.enter_context(tc.psum_pool(name="psum", bufs=1))
 
         offsets = keep.tile([P, S // 16], U16, name="offsets")
         x_rows = xT.rearrange("(g p j) t -> g j p t", p=P, j=PACK)
         w_rows = w1.rearrange("(g p j) n -> g p j n", p=P, j=PACK)
-        x_planes = [keep.tile([P, T], F32, name="x_plane%d" % i) for i in range(PASSES * PACK)]
-        w_raw = [keep.tile([P, PACK, N], F32, name="w_raw%d" % g) for g in range(PASSES)]
+        x_pair = shared.tile([P, 2 * T], F32, name="x_pair", offset=0, align_bytes=64)
+        x_planes = [keep.tile([P, T], F32, name="x_first%d" % j)[:] for j in range(2)]
+        x_planes = x_planes + [x_pair[:, j * T : (j + 1) * T] for j in range(2)]
+        x_planes = x_planes + [keep.tile([P, T], F32, name="x_plane%d" % j, align_bytes=64)[:] for j in range(PACK)]
+        w_pieces = [(0, 0, N), (1, 0, N // 2), (1, N // 2, N)]
+        w_raw = [keep.tile([P, PACK, hi - lo], F32, name="w_raw%d_%d" % (g, lo)) for g, lo, hi in w_pieces]
         stat_runs = keep.tile([P, RUN + P], F32, name="stat_runs")
         gsum_col = keep.tile([P, 2], F32, name="gsum_col")
         b_col = keep.tile([P, 2], F32, name="b_col")
 
         def load_x(i):
-            nc.sync.dma_start(out=x_planes[i][:], in_=x_rows[i // PACK, i % PACK])
+            nc.sync.dma_start(out=x_planes[i], in_=x_rows[i // PACK, i % PACK])
+
+        def load_w(i):
+            g, lo, hi = w_pieces[i]
+            nc.sync.dma_start(out=w_raw[i][:], in_=w_rows[g][:, :, lo:hi])
 
         load_x(0)
         nc.sync.dma_start(offsets[:], offs)
-        nc.scalar.dma_start(out=stat_runs[:, 0:RUN], in_=mean[0:1, :].rearrange("o (p c) -> (o p) c", c=RUN))
-        nc.scalar.dma_start(out=stat_runs[:, RUN : 2 * RUN], in_=inv[0:1, :].rearrange("o (p c) -> (o p) c", c=RUN))
-        nc.scalar.dma_start(out=gsum_col[:], in_=gsum.rearrange("(p t) o -> p (t o)", t=2))
-        nc.scalar.dma_start(out=b_col[:], in_=b.rearrange("(p t) o -> p (t o)", t=2))
-        for i in range(1, PACK):
-            load_x(i)
-        nc.sync.dma_start(out=w_raw[0][:], in_=w_rows[0])
+        nc.sync.dma_start(out=stat_runs[:, 0:RUN], in_=mean[0:1, :].rearrange("o (p c) -> (o p) c", c=RUN))
+        nc.sync.dma_start(out=stat_runs[:, RUN : 2 * RUN], in_=inv[0:1, :].rearrange("o (p c) -> (o p) c", c=RUN))
+        nc.sync.dma_start(out=gsum_col[:], in_=gsum.rearrange("(p t) o -> p (t o)", t=2))
+        nc.sync.dma_start(out=b_col[:], in_=b.rearrange("(p t) o -> p (t o)", t=2))
+        load_x(1)
+        nc.sync.dma_start(out=x_pair[:], in_=xT[0:K_PASS, :].rearrange("(p u j) t -> u p (j t)", u=2, j=2)[1])
+        load_w(0)
         for i in range(PACK, 2 * PACK):
             load_x(i)
-        nc.sync.dma_start(out=w_raw[1][:], in_=w_rows[1])
+        load_w(1)
+        load_w(2)
 
         ident = keep.tile([P, P], F32, name="ident")
         make_identity(nc, ident[:])
@@ -73,23 +83,31 @@ def tile_picked_lnfold_silu_l_kernel(tc, xT, mean, inv, gsum, b, w1, offs, out):
                 bank[:].rearrange("p c n -> p n c"),
             )
 
-        x_grouped = [keep.tile([P, S, PACK], BF16, name="x_grouped%d" % g, align_bytes=64) for g in range(PASSES)]
+        x_grouped = {
+            (0, 0): keep.tile([P, S, PACK], BF16, name="x_grouped0", align_bytes=64),
+            (1, 0): shared.tile([P, HALF, PACK], BF16, name="x_grouped1a", offset=0, align_bytes=64),
+            (1, HALF): shared.tile([P, HALF, PACK], BF16, name="x_grouped1b", offset=2048, align_bytes=64),
+        }
         x_picked = keep.tile([P, PACK, S], F32, name="x_picked")
         x_codes = {}
         x_scales = {}
-        w_grouped = [keep.tile([P, N, PACK], BF16, name="w_grouped%d" % g, align_bytes=64) for g in range(PASSES)]
-        w_codes = [keep.tile([P, N], U32, name="w_codes%d" % g, align_bytes=64) for g in range(PASSES)]
+        stat_picked = keep.tile([P, S], F32, name="stat_picked", align_bytes=64)
+        w_grouped = [
+            keep.tile([P, N, PACK], BF16, name="w_grouped0", tag="stat_picked", align_bytes=64),
+            keep.tile([P, N, PACK], BF16, name="w_grouped1", align_bytes=64),
+        ]
+        w_codes = {}
         w_scales = [keep.tile([P, N], U8, name="w_scales%d" % g, align_bytes=64) for g in range(PASSES)]
         acc = [psum.tile([P, N], F32, name="acc%d" % blk) for blk in range(BLOCKS)]
 
         def gather_x(i, lo, hi):
             nc.vector.tensor_copy(
-                x_grouped[i // PACK][:, lo:hi, i % PACK],
-                x_planes[i][:].indirect(offsets[:, lo // 16 : hi // 16]),
+                x_grouped[i // PACK, lo][:, :, i % PACK],
+                x_planes[i].indirect(offsets[:, lo // 16 : hi // 16]),
             )
 
         def pick_x(j):
-            nc.vector.tensor_copy(x_picked[:, j, :], x_planes[j][:].indirect(offsets[:]))
+            nc.vector.tensor_copy(x_picked[:, j, :], x_planes[j].indirect(offsets[:]))
 
         def quantize_x(g, lo, hi, tag):
             codes = keep.tile([P, hi - lo], U32, name="x_codes", tag=tag, align_bytes=64)
@@ -97,20 +115,22 @@ def tile_picked_lnfold_silu_l_kernel(tc, xT, mean, inv, gsum, b, w1, offs, out):
             nc.vector.quantize_mx(
                 out=codes[:].bitcast(FP8X4),
                 scales=scales[:],
-                in_=x_grouped[g][:].rearrange("p s j -> p (s j)")[:, PACK * lo : PACK * hi],
+                in_=x_grouped[g, lo][:].rearrange("p s j -> p (s j)"),
             )
             for blk in range(lo // P, hi // P):
                 cols = slice(blk * P - lo, (blk + 1) * P - lo)
                 x_codes[g, blk] = codes[:, cols]
                 x_scales[g, blk] = scales[:, cols]
 
-        def group_w(g):
+        def group_w(piece):
+            g, lo, hi = w_pieces[piece]
             nc.scalar.copy(
-                w_grouped[g][:].rearrange("p (c i) j -> p c j i", i=4),
-                w_raw[g][:].rearrange("p j (c i) -> p c j i", i=4),
+                w_grouped[g][:, lo:hi, :].rearrange("p (c i) j -> p c j i", i=4),
+                w_raw[piece][:].rearrange("p j (c i) -> p c j i", i=4),
             )
 
-        def quantize_w(g):
+        def quantize_w(g, codes):
+            w_codes[g] = codes
             nc.vector.quantize_mx(
                 out=w_codes[g][:].bitcast(FP8X4),
                 scales=w_scales[g][:],
@@ -129,7 +149,6 @@ def tile_picked_lnfold_silu_l_kernel(tc, xT, mean, inv, gsum, b, w1, offs, out):
             )
 
         pick_x(0)
-        stat_picked = keep.tile([P, S], F32, name="stat_picked")
         nc.vector.tensor_copy(stat_picked[:], stat_window[:].indirect(offsets[:]))
         stat_turned = psum.tile([P, BLOCKS, P], F32, name="stat_turned", tag="turn0")
         for blk in range(BLOCKS):
@@ -140,50 +159,56 @@ def tile_picked_lnfold_silu_l_kernel(tc, xT, mean, inv, gsum, b, w1, offs, out):
         for t in range(2):
             nc.tensor.transpose(spread[:, 0, t, :], gsum_col[:, t : t + 1].to_broadcast([P, P]), ident[:])
             nc.tensor.transpose(spread[:, 1, t, :], b_col[:, t : t + 1].to_broadcast([P, P]), ident[:])
-        rows = keep.tile([P, 2, N], F32, name="rows")
-        nc.scalar.copy(rows[:].rearrange("p v (n t) -> p v n t", t=2), spread[:].rearrange("p v t n -> p v n t"))
+        rows = x_picked[:, 2:4, 0:N]
+        nc.scalar.copy(rows.rearrange("p v (n t) -> p v n t", t=2), spread[:].rearrange("p v t n -> p v n t"))
 
         pick_x(1)
         shift = keep.tile([P, BLOCKS], F32, name="shift")
         nc.vector.scalar_tensor_tensor(shift[:], stats[:, :, 0], -1.0, stats[:, :, 1], MULT, MULT)
-        pick_x(2)
         offset_term = [keep.tile([P, N], F32, name="offset_term%d" % blk) for blk in range(BLOCKS)]
         for blk in range(BLOCKS):
             nc.vector.scalar_tensor_tensor(
                 offset_term[blk][:], rows[:, 0, :], shift[:, blk : blk + 1], rows[:, 1, :], MULT, ADD
             )
+        pick_x(2)
         pick_x(3)
+        group_w(0)
         nc.scalar.copy(
-            x_grouped[0][:].rearrange("p (c i) j -> p c j i", i=4),
+            x_grouped[0, 0][:].rearrange("p (c i) j -> p c j i", i=4),
             x_picked[:].rearrange("p j (c i) -> p c j i", i=4),
         )
-        group_w(0)
-        gather_x(4, 0, S)
-        quantize_x(0, 0, S, "x_codes0")
-        quantize_w(0)
+        gather_x(4, 0, HALF)
+        gather_x(4, HALF, S)
+        quantize_w(0, keep.tile([P, N], U32, name="w_codes0", tag="x_plane0", align_bytes=64))
+        gather_x(5, 0, HALF)
+        gather_x(5, HALF, S)
+        quantize_x(0, 0, S, "x_plane1")
         for blk in range(BLOCKS):
             multiply(0, blk)
-        gather_x(5, 0, S)
-        gather_x(6, 0, S)
+        gather_x(6, 0, HALF)
+        gather_x(6, HALF, S)
         gather_x(7, 0, HALF)
         gather_x(7, HALF, S)
         group_w(1)
+        group_w(2)
         quantize_x(1, 0, HALF, "x_codes1")
-        quantize_w(1)
+        quantize_w(1, shared.tile([P, N], U32, name="w_codes1", offset=0, align_bytes=64))
         quantize_x(1, HALF, S, "w_grouped1")
         for blk in range(BLOCKS):
             multiply(1, blk)
 
         out_view = out.rearrange("(t p) s -> p t s", p=P)
-        for blk in range(BLOCKS):
-            pre = keep.tile([P, N], F32, name="pre%d" % blk)
+        pieces = [(0, 0, 1), (0, 1, 2), (1, 0, 2), (2, 0, 2), (3, 0, 1), (3, 1, 2)]
+        banks = ["turn0", "turn1", "turn2", "turn3", "acc0", "acc1"]
+        for (blk, t0, t1), bank_tag in zip(pieces, banks):
+            cols = slice(t0 * P, t1 * P)
+            pre = keep.tile([P, (t1 - t0) * P], F32, name="pre%d_%d" % (blk, t0))
             nc.vector.scalar_tensor_tensor(
-                pre[:], acc[blk][:], stats[:, blk, 1:2], offset_term[blk][:], MULT, ADD
+                pre[:], acc[blk][:, cols], stats[:, blk, 1:2], offset_term[blk][:, cols], MULT, ADD
             )
-            turned = psum.tile([P, 2, P], F32, name="turned%d" % blk, tag="turn%d" % blk)
-            for t in range(2):
+            turned = psum.tile([P, t1 - t0, P], F32, name="turned", tag=bank_tag)
+            for t in range(t1 - t0):
                 nc.tensor.transpose(turned[:, t, :], pre[:, t * P : (t + 1) * P], ident[:])
-            result = keep.tile([P, 2, P], F32, name="result%d" % blk)
+            result = keep.tile([P, t1 - t0, P], F32, name="result%d_%d" % (blk, t0))
             nc.scalar.activation(result[:], turned[:], SILU)
-            queue = nc.scalar if blk == BLOCKS - 1 else nc.sync
-            queue.dma_start(out=out_view[:, :, blk * P : (blk + 1) * P], in_=result[:])
+            nc.sync.dma_start(out=out_view[:, t0:t1, blk * P : (blk + 1) * P], in_=result[:])

from contextlib import ExitStack

import concourse.mybir as mybir
from concourse.masks import make_identity

K, T, S, N = 1024, 2048, 512, 256
FLOPS = 2 * K * S * N
BYTES = 4 * (K * T + 2 * T + 2 * N + K * N + N * S) + 2 * 128 * (S // 16)

F32 = mybir.dt.float32
BF16 = mybir.dt.bfloat16
U32 = mybir.dt.uint32
U16 = mybir.dt.uint16
U8 = mybir.dt.uint8
FP8X4 = mybir.dt.float8_e4m3fn_x4
MULT = mybir.AluOpType.mult
ADD = mybir.AluOpType.add
SILU = mybir.ActivationFunctionType.Silu

P = 128
PACK = 4
K_PASS = P * PACK
PASSES = K // K_PASS
BLOCKS = S // P
HALF = S // 2
RUN = T // P


def tile_picked_lnfold_silu_l_kernel(tc, xT, mean, inv, gsum, b, w1, offs, out):
    nc = tc.nc
    with ExitStack() as ctx:
        keep = ctx.enter_context(tc.tile_pool(name="keep", bufs=1))
        shared = ctx.enter_context(tc.tile_pool(name="shared", bufs=1))
        psum = ctx.enter_context(tc.psum_pool(name="psum", bufs=1))

        offsets = keep.tile([P, S // 16], U16, name="offsets")
        x_rows = xT.rearrange("(g p j) t -> g j p t", p=P, j=PACK)
        w_rows = w1.rearrange("(g p j) n -> g p j n", p=P, j=PACK)
        x_pair = shared.tile([P, 2 * T], F32, name="x_pair", offset=0, align_bytes=64)
        x_planes = [keep.tile([P, T], F32, name="x_first%d" % j)[:] for j in range(2)]
        x_planes = x_planes + [x_pair[:, j * T : (j + 1) * T] for j in range(2)]
        x_planes = x_planes + [keep.tile([P, T], F32, name="x_plane%d" % j, align_bytes=64)[:] for j in range(PACK)]
        w_pieces = [(0, 0, N), (1, 0, N // 2), (1, N // 2, N)]
        w_raw = [keep.tile([P, PACK, hi - lo], F32, name="w_raw%d_%d" % (g, lo)) for g, lo, hi in w_pieces]
        stat_runs = keep.tile([P, RUN + P], F32, name="stat_runs")
        gsum_col = keep.tile([P, 2], F32, name="gsum_col")
        b_col = keep.tile([P, 2], F32, name="b_col")

        def load_x(i):
            nc.sync.dma_start(out=x_planes[i], in_=x_rows[i // PACK, i % PACK])

        def load_w(i):
            g, lo, hi = w_pieces[i]
            nc.sync.dma_start(out=w_raw[i][:], in_=w_rows[g][:, :, lo:hi])

        load_x(0)
        nc.sync.dma_start(offsets[:], offs)
        nc.sync.dma_start(out=stat_runs[:, 0:RUN], in_=mean[0:1, :].rearrange("o (p c) -> (o p) c", c=RUN))
        nc.sync.dma_start(out=stat_runs[:, RUN : 2 * RUN], in_=inv[0:1, :].rearrange("o (p c) -> (o p) c", c=RUN))
        nc.sync.dma_start(out=gsum_col[:], in_=gsum.rearrange("(p t) o -> p (t o)", t=2))
        nc.sync.dma_start(out=b_col[:], in_=b.rearrange("(p t) o -> p (t o)", t=2))
        load_x(1)
        nc.sync.dma_start(out=x_pair[:], in_=xT[0:K_PASS, :].rearrange("(p u j) t -> u p (j t)", u=2, j=2)[1])
        load_w(0)
        for i in range(PACK, 2 * PACK):
            load_x(i)
        load_w(1)
        load_w(2)

        ident = keep.tile([P, P], F32, name="ident")
        make_identity(nc, ident[:])
        warm = keep.tile([P, 1], F32, name="warm")
        nc.scalar.activation(warm[:], ident[:, 0:1], SILU)

        stat_window = keep.tile([P, T], F32, name="stat_window")
        nc.vector.memset(stat_runs[:, 2 * RUN :], 0.0)
        for q in range(RUN // 4):
            bank = psum.tile([P, 4, P], F32, name="bank", tag="turn%d" % q)
            for c in range(4):
                nc.tensor.transpose(bank[:, c, :], stat_runs[:, 4 * q + c : 4 * q + c + P], ident[:])
            nc.scalar.copy(
                stat_window[:].rearrange("p (n c) -> p n c", c=RUN)[:, :, 4 * q : 4 * q + 4],
                bank[:].rearrange("p c n -> p n c"),
            )

        x_grouped = {
            (0, 0): keep.tile([P, S, PACK], BF16, name="x_grouped0", align_bytes=64),
            (1, 0): shared.tile([P, HALF, PACK], BF16, name="x_grouped1a", offset=0, align_bytes=64),
            (1, HALF): shared.tile([P, HALF, PACK], BF16, name="x_grouped1b", offset=2048, align_bytes=64),
        }
        x_picked = keep.tile([P, PACK, S], F32, name="x_picked")
        x_codes = {}
        x_scales = {}
        stat_picked = keep.tile([P, S], F32, name="stat_picked", align_bytes=64)
        w_grouped = [
            keep.tile([P, N, PACK], BF16, name="w_grouped0", tag="stat_picked", align_bytes=64),
            keep.tile([P, N, PACK], BF16, name="w_grouped1", align_bytes=64),
        ]
        w_codes = {}
        w_scales = [keep.tile([P, N], U8, name="w_scales%d" % g, align_bytes=64) for g in range(PASSES)]
        acc = [psum.tile([P, N], F32, name="acc%d" % blk) for blk in range(BLOCKS)]

        def gather_x(i, lo, hi):
            nc.vector.tensor_copy(
                x_grouped[i // PACK, lo][:, :, i % PACK],
                x_planes[i].indirect(offsets[:, lo // 16 : hi // 16]),
            )

        def pick_x(j):
            nc.vector.tensor_copy(x_picked[:, j, :], x_planes[j].indirect(offsets[:]))

        def quantize_x(g, lo, hi, tag):
            codes = keep.tile([P, hi - lo], U32, name="x_codes", tag=tag, align_bytes=64)
            scales = keep.tile([P, hi - lo], U8, name="x_scales", tag="x_scales%d_%d" % (g, lo), align_bytes=64)
            nc.vector.quantize_mx(
                out=codes[:].bitcast(FP8X4),
                scales=scales[:],
                in_=x_grouped[g, lo][:].rearrange("p s j -> p (s j)"),
            )
            for blk in range(lo // P, hi // P):
                cols = slice(blk * P - lo, (blk + 1) * P - lo)
                x_codes[g, blk] = codes[:, cols]
                x_scales[g, blk] = scales[:, cols]

        def group_w(piece):
            g, lo, hi = w_pieces[piece]
            nc.scalar.copy(
                w_grouped[g][:, lo:hi, :].rearrange("p (c i) j -> p c j i", i=4),
                w_raw[piece][:].rearrange("p j (c i) -> p c j i", i=4),
            )

        def quantize_w(g, codes):
            w_codes[g] = codes
            nc.vector.quantize_mx(
                out=w_codes[g][:].bitcast(FP8X4),
                scales=w_scales[g][:],
                in_=w_grouped[g][:].rearrange("p n j -> p (n j)"),
            )

        def multiply(g, blk):
            nc.tensor.matmul_mx(
                out=acc[blk][:],
                lhsT=x_codes[g, blk].bitcast(FP8X4),
                lhsT_scale=x_scales[g, blk],
                rhs=w_codes[g][:].bitcast(FP8X4),
                rhs_scale=w_scales[g][:],
                start=(g == 0),
                stop=(g == PASSES - 1),
            )

        pick_x(0)
        nc.vector.tensor_copy(stat_picked[:], stat_window[:].indirect(offsets[:]))
        stat_turned = psum.tile([P, BLOCKS, P], F32, name="stat_turned", tag="turn0")
        for blk in range(BLOCKS):
            nc.tensor.transpose(stat_turned[:, blk, :], stat_picked[:, blk * P : (blk + 1) * P], ident[:])
        stats = keep.tile([P, BLOCKS, 2], F32, name="stats")
        nc.scalar.copy(stats[:], stat_turned[:, :, 0 : 2 * RUN : RUN])
        spread = psum.tile([P, 2, 2, P], F32, name="spread", tag="turn1")
        for t in range(2):
            nc.tensor.transpose(spread[:, 0, t, :], gsum_col[:, t : t + 1].to_broadcast([P, P]), ident[:])
            nc.tensor.transpose(spread[:, 1, t, :], b_col[:, t : t + 1].to_broadcast([P, P]), ident[:])
        rows = x_picked[:, 2:4, 0:N]
        nc.scalar.copy(rows.rearrange("p v (n t) -> p v n t", t=2), spread[:].rearrange("p v t n -> p v n t"))

        pick_x(1)
        shift = keep.tile([P, BLOCKS], F32, name="shift")
        nc.vector.scalar_tensor_tensor(shift[:], stats[:, :, 0], -1.0, stats[:, :, 1], MULT, MULT)
        offset_term = [keep.tile([P, N], F32, name="offset_term%d" % blk) for blk in range(BLOCKS)]
        for blk in range(BLOCKS):
            nc.vector.scalar_tensor_tensor(
                offset_term[blk][:], rows[:, 0, :], shift[:, blk : blk + 1], rows[:, 1, :], MULT, ADD
            )
        pick_x(2)
        pick_x(3)
        group_w(0)
        nc.scalar.copy(
            x_grouped[0, 0][:].rearrange("p (c i) j -> p c j i", i=4),
            x_picked[:].rearrange("p j (c i) -> p c j i", i=4),
        )
        gather_x(4, 0, HALF)
        gather_x(4, HALF, S)
        quantize_w(0, keep.tile([P, N], U32, name="w_codes0", tag="x_plane0", align_bytes=64))
        gather_x(5, 0, HALF)
        gather_x(5, HALF, S)
        quantize_x(0, 0, S, "x_plane1")
        for blk in range(BLOCKS):
            multiply(0, blk)
        gather_x(6, 0, HALF)
        gather_x(6, HALF, S)
        gather_x(7, 0, HALF)
        gather_x(7, HALF, S)
        group_w(1)
        group_w(2)
        quantize_x(1, 0, HALF, "x_codes1")
        quantize_w(1, shared.tile([P, N], U32, name="w_codes1", offset=0, align_bytes=64))
        quantize_x(1, HALF, S, "w_grouped1")
        for blk in range(BLOCKS):
            multiply(1, blk)

        out_view = out.rearrange("(t p) s -> p t s", p=P)
        pieces = [(0, 0, 1), (0, 1, 2), (1, 0, 2), (2, 0, 2), (3, 0, 1), (3, 1, 2)]
        banks = ["turn0", "turn1", "turn2", "turn3", "acc0", "acc1"]
        for (blk, t0, t1), bank_tag in zip(pieces, banks):
            cols = slice(t0 * P, t1 * P)
            pre = keep.tile([P, (t1 - t0) * P], F32, name="pre%d_%d" % (blk, t0))
            nc.vector.scalar_tensor_tensor(
                pre[:], acc[blk][:, cols], stats[:, blk, 1:2], offset_term[blk][:, cols], MULT, ADD
            )
            turned = psum.tile([P, t1 - t0, P], F32, name="turned", tag=bank_tag)
            for t in range(t1 - t0):
                nc.tensor.transpose(turned[:, t, :], pre[:, t * P : (t + 1) * P], ident[:])
            result = keep.tile([P, t1 - t0, P], F32, name="result%d_%d" % (blk, t0))
            nc.scalar.activation(result[:], turned[:], SILU)
            nc.sync.dma_start(out=out_view[:, t0:t1, blk * P : (blk + 1) * P], in_=result[:])
